import numpy as np
import ml_dtypes


def mxq(x, axis, fmt="e4m3"):
    dtype, down = {"e4m3": (ml_dtypes.float8_e4m3fn, 7), "e5m2": (ml_dtypes.float8_e5m2, 14)}[fmt]
    v = np.moveaxis(np.asarray(x, np.float32).astype(ml_dtypes.bfloat16).astype(np.float64), axis, -1)
    blocks = v.reshape(v.shape[:-1] + (-1, 32))
    amax = np.abs(blocks).max(-1, keepdims=True)
    byte = np.maximum(np.where(amax > 0, np.frexp(amax)[1] - 1 + 127, 0) - down, 1)
    scale = np.exp2(byte - 127.0)
    codes = (blocks / scale).astype(np.float32).astype(dtype).astype(np.float64)
    return np.moveaxis((codes * scale).reshape(v.shape), -1, axis)


WIDE = False


def mx_kscale(k):
    if not WIDE:
        return np.ones(k)
    levels = np.array([10, -10, 5, -5, 0])
    if k % 512:
        return np.exp2(np.random.permutation(np.resize(levels, k // 32))).repeat(32)
    a = np.empty((k // 512, 16))
    for p in range(k // 512):
        a[p, :8] = np.random.permutation(np.resize(levels, 8))
        for g in range(8):
            far = levels[np.abs(levels - a[p, g]) >= 10]
            a[p, g + 8] = far[np.random.randint(len(far))]
    return np.exp2(a.ravel()).repeat(32)


def f64(x):
    return np.asarray(x).astype(np.float64)


def striped(idx):
    return np.tile(idx.reshape(-1, 16).T, (8, 1)).astype(np.uint16)


def unstriped(offs):
    return offs[:16].T.reshape(-1).astype(np.int64)


def pack_weight(w):
    k, n = w.shape
    w = f64(np.asarray(w, np.float32).astype(ml_dtypes.bfloat16)).reshape(k // 32, 32, n)
    amax = np.abs(w).max(1)
    byte = np.clip(np.where(amax > 0, np.frexp(amax)[1] - 1 + 127 - 7, 1), 1, 254)
    scaled = (w * np.exp2(127.0 - byte)[:, None, :]).reshape(k, n).astype(np.float32)
    words = np.ascontiguousarray(scaled.reshape(k // 512, 128, 4, n).transpose(0, 1, 3, 2)).astype(ml_dtypes.float8_e4m3fn).view(np.uint8)
    return words, np.ascontiguousarray(byte.astype(np.uint8).reshape(k // 512, 16, n))


def unpack_weight(words, scales):
    g, p, n, _ = words.shape
    vals = np.ascontiguousarray(words).view(ml_dtypes.float8_e4m3fn).astype(np.float64) * np.repeat(np.exp2(scales.astype(np.float64) - 127.0), 8, axis=1)[..., None]
    return vals.transpose(0, 1, 3, 2).reshape(g * 512, n)


def sigmoid(v):
    return 1.0 / (1.0 + np.exp(-np.maximum(v, -700.0)))


K, T, S, D, N = 1024, 4096, 1024, 2, 128
P = 2 ** 7


def setup_inputs():
    n = np.random.standard_normal
    s = mx_kscale(K)[:, None]
    packed_xT = pack_weight(n((K, T)) * s)
    return {
        "x_words": packed_xT[0],
        "x_scales": packed_xT[1],
        "w1": (n((K, N)) / np.sqrt(K) / s).astype(np.float32),
        "prior": (np.tile(n(S) * 0.7, (P, 1))).astype(np.float32),
        "wgt": (np.tile(np.random.uniform(0.3, 0.95, S), (P, 1))).astype(np.float32),
        "offs": striped(np.random.permutation(T)[:S]),
    }


def reference(x_words, x_scales, w1, prior, wgt, offs):
    xq = unpack_weight(x_words, x_scales)[:, unstriped(offs)]
    y = mxq(f64(w1), 0, "e4m3").T @ xq
    t1 = y - 0.8
    t0 = 1.2 * (y + 0.3)
    post = sigmoid(-0.7 * ((t1) ** 2) - (-1.0 * (t0 + np.exp(-1.0 * t0))) + f64(prior)[:1])
    lg = np.log(-1.0 * (post * f64(wgt)[:1]) + 1.0)
    return -1.0 * (lg.reshape(len(lg), -1, D).sum(axis=2))

@@ -1,0 +1,162 @@
+import math
+from contextlib import ExitStack
+
+import concourse.mybir as mybir
+from concourse.masks import make_identity
+
+K, T, S, N = 1024, 4096, 1024, 128
+P = 128
+PASSES = K // 512
+FLOPS = 2 * K * S * N
+
+F32 = mybir.dt.float32
+BF16 = mybir.dt.bfloat16
+I32 = mybir.dt.int32
+U32 = mybir.dt.uint32
+U16 = mybir.dt.uint16
+U8 = mybir.dt.uint8
+FP8X4 = mybir.dt.float8_e4m3fn_x4
+ACT = mybir.ActivationFunctionType
+ALU = mybir.AluOpType
+
+GATHER = 512
+BLOCK = 256
+BLOCKS = S // BLOCK
+
+CENTRE = (2 * 0.7 * 0.8 + 1.2) / (2 * 0.7)
+OFFSET = 0.7 * CENTRE * CENTRE - 0.7 * 0.8 * 0.8 + 1.2 * 0.3
+
+
+def tile_picked_yprot_nlog_p_kernel(tc, x_words, x_scales, w1, prior, wgt, offs, out):
+    nc = tc.nc
+    with ExitStack() as ctx:
+        keep = ctx.enter_context(tc.tile_pool(name="keep", bufs=1))
+        psum = ctx.enter_context(tc.psum_pool(name="psum", bufs=1))
+
+        offsets = keep.tile([P, S // 16], U16, name="offsets")
+        nc.sync.dma_start(offsets[:], offs)
+
+        scale_table = keep.tile([P, T], U8, name="scale_table", align_bytes=64)
+        nc.sync.dma_start(scale_table[0:32, :].bitcast(I32), x_scales.rearrange("o i c -> (o i) c").bitcast(I32))
+        nc.gpsimd.memset(scale_table[32:64, :].bitcast(I32), 0)
+        nc.vector.memset(scale_table[64:P, :].bitcast(I32), 0)
+
+        rows = []
+        for name, source in (("prior", prior), ("wgt", wgt)):
+            row = keep.tile([P, 2, 4], F32, name=name + "_row")
+            nc.scalar.dma_start(row[:], source[0].rearrange("(h n m) -> n h m", h=2, m=4))
+            rows.append(row)
+
+        w_raw = keep.tile([P, PASSES, 4, N], F32, name="w_raw")
+        nc.sync.dma_start(w_raw[:], w1.rearrange("(o p j) n -> p o j n", o=PASSES, j=4))
+
+        word_table = []
+        for o in range(PASSES):
+            table = keep.tile([P, T], I32, name="word_table%d" % o, align_bytes=64)
+            nc.sync.dma_start(table[:], x_words[o].rearrange("p c r -> p (c r)").bitcast(I32))
+            word_table.append(table)
+
+        identity = keep.tile([P, P], F32, name="identity")
+        make_identity(nc, identity[:])
+        spread = []
+        for index, row in enumerate(rows):
+            banks = []
+            for h in range(2):
+                bank = psum.tile([P, 4, P], F32, name="spread%d_%d" % (index, h))
+                for m in range(4):
+                    nc.tensor.transpose(bank[:, m, :], row[:, h, m : m + 1].to_broadcast([P, P]), identity[:])
+                banks.append(bank)
+            spread.append(banks)
+
+        def spread_block(index, b):
+            n0 = (b % 2) * (BLOCK // 4)
+            return spread[index][b // 2][:].rearrange("p m n -> p n m")[:, n0 : n0 + BLOCK // 4, :]
+
+        def by_four(ap):
+            return ap.rearrange("p (n m) -> p n m", m=4)
+
+        w_bf = keep.tile([P, PASSES * N * 4], BF16, name="w_bf", align_bytes=64)
+        nc.scalar.activation(
+            w_bf[:].rearrange("p (o n j) -> p o n j", o=PASSES, j=4),
+            w_raw[:].rearrange("p o j n -> p o n j"),
+            ACT.Copy,
+        )
+
+        picked_bytes = keep.tile([P, S], U8, name="picked_bytes", align_bytes=64)
+        nc.vector.tensor_copy(picked_bytes[:], scale_table[:].indirect(offsets[:]))
+        planes = keep.tile([P, S], U8, name="planes", align_bytes=64)
+        nc.vector.tensor_copy(planes[:].bitcast(I32), picked_bytes[:].bitcast(I32))
+        for o in range(PASSES):
+            for q in range(4):
+                source, target = 16 * o + 4 * q, 32 * q + 4 * o
+                if source != target:
+                    nc.scalar.dma_start(
+                        planes[target : target + 4, :].bitcast(I32), picked_bytes[source : source + 4, :].bitcast(I32)
+                    )
+
+        w_codes = keep.tile([P, PASSES * N], U32, name="w_codes", align_bytes=64)
+        w_scales = keep.tile([P, PASSES * N], U8, name="w_scales", align_bytes=64)
+        nc.vector.quantize_mx(w_codes[:].bitcast(FP8X4), w_scales[:], w_bf[:])
+
+        y = [psum.tile([P, BLOCK], F32, name="y%d" % b) for b in range(BLOCKS)]
+        for o in range(PASSES):
+            for g in range(S // GATHER):
+                picked = keep.tile([P, GATHER], U32, name="picked%d_%d" % (o, g), align_bytes=64)
+                nc.vector.tensor_copy(
+                    picked[:],
+                    word_table[o][:].bitcast(U32).indirect(offsets[:, g * GATHER // 16 : (g + 1) * GATHER // 16]),
+                )
+                for i in range(GATHER // BLOCK):
+                    b = g * (GATHER // BLOCK) + i
+                    nc.tensor.matmul_mx(
+                        y[b][:],
+                        lhsT=w_codes[:, o * N : (o + 1) * N].bitcast(FP8X4),
+                        lhsT_scale=w_scales[:, o * N : (o + 1) * N],
+                        rhs=picked[:, i * BLOCK : (i + 1) * BLOCK].bitcast(FP8X4),
+                        rhs_scale=planes[4 * o : P, b * BLOCK : (b + 1) * BLOCK],
+                        start=(o == 0),
+                        stop=(o == PASSES - 1),
+                    )
+
+        def cols(b):
+            return slice(b * BLOCK, (b + 1) * BLOCK)
+
+        def fresh(name, b, width=BLOCK):
+            return keep.tile([P, width], F32, name="%s%d" % (name, b))
+
+        root = math.sqrt(0.7)
+        square, expo, part, logit, th = {}, {}, {}, {}, {}
+        for b in range(BLOCKS):
+            square[b] = fresh("square", b)
+            nc.scalar.activation(square[b][:], y[b][:], ACT.Square, bias=-root * CENTRE, scale=root)
+            expo[b] = fresh("expo", b)
+            nc.scalar.activation(expo[b][:], y[b][:], ACT.Exp, bias=-1.2 * 0.3, scale=-1.2)
+        for pair in range(BLOCKS // 2):
+            for b in (2 * pair, 2 * pair + 1):
+                part[b] = fresh("part", b)
+                nc.vector.tensor_tensor(by_four(part[b][:]), spread_block(0, b), by_four(square[b][:]), ALU.subtract)
+            for b in (2 * pair, 2 * pair + 1):
+                logit[b] = fresh("logit", b)
+                nc.vector.tensor_tensor(logit[b][:], part[b][:], expo[b][:], ALU.add)
+        for b in range(BLOCKS):
+            th[b] = fresh("th", b)
+            nc.scalar.activation(th[b][:], logit[b][:], ACT.Tanh, bias=0.5 * OFFSET, scale=0.5)
+
+        HALF = 2 * BLOCK
+        for h in range(S // HALF):
+            twice_p = fresh("twice_p", h, HALF)
+            for i in range(2):
+                b = 2 * h + i
+                nc.vector.scalar_tensor_tensor(
+                    by_four(twice_p[:, cols(i)]), by_four(th[b][:]), 1.0, spread_block(1, b), ALU.add, ALU.mult
+                )
+            pairs = twice_p[:].rearrange("p (v d) -> p v d", d=2)
+            cross = fresh("cross", h)
+            nc.vector.scalar_tensor_tensor(cross[:], pairs[:, :, 0], -2.0, pairs[:, :, 1], ALU.add, ALU.mult)
+            excess = fresh("excess", h)
+            nc.vector.scalar_tensor_tensor(excess[:], pairs[:, :, 0], -2.0, cross[:], ALU.mult, ALU.add)
+            log_q = keep.tile([P, BLOCK], F32, name="logit%d" % (BLOCKS - 1 - h))
+            nc.scalar.activation(log_q[:], excess[:], ACT.Ln, bias=1.0, scale=0.25)
+            result = fresh("result", h)
+            nc.vector.tensor_scalar(result[:], log_q[:], -1.0, None, ALU.mult)
+            nc.sync.dma_start(out[:, cols(h)], result[:])

@@ -2,11 +2,11 @@ import math
 from contextlib import ExitStack
 
 import concourse.mybir as mybir
-from concourse.masks import make_identity
 
 K, T, S, N = 1024, 4096, 1024, 128
 P = 128
-PASSES = K // 512
+PACK = 4
+PASSES = K // (P * PACK)
 FLOPS = 2 * K * S * N
 
 F32 = mybir.dt.float32
@@ -19,9 +19,14 @@ FP8X4 = mybir.dt.float8_e4m3fn_x4
 ACT = mybir.ActivationFunctionType
 ALU = mybir.AluOpType
 
+STRIPE = 16
+QUADRANT = 32
+ROWS = 4
 GATHER = 512
 BLOCK = 256
 BLOCKS = S // BLOCK
+PER_GATHER = GATHER // BLOCK
+PROTEINS = BLOCK // 2
 
 CENTRE = (2 * 0.7 * 0.8 + 1.2) / (2 * 0.7)
 OFFSET = 0.7 * CENTRE * CENTRE - 0.7 * 0.8 * 0.8 + 1.2 * 0.3
@@ -33,22 +38,22 @@ def tile_picked_yprot_nlog_p_kernel(tc, x_words, x_scales, w1, prior, wgt, offs,
         keep = ctx.enter_context(tc.tile_pool(name="keep", bufs=1))
         psum = ctx.enter_context(tc.psum_pool(name="psum", bufs=1))
 
-        offsets = keep.tile([P, S // 16], U16, name="offsets")
+        def cols(b):
+            return slice(b * BLOCK, (b + 1) * BLOCK)
+
+        def fresh(name, index, width=BLOCK):
+            return keep.tile([P, width], F32, name="%s%d" % (name, index))
+
+        offsets = keep.tile([P, S // STRIPE], U16, name="offsets")
         nc.sync.dma_start(offsets[:], offs)
 
-        scale_table = keep.tile([P, T], U8, name="scale_table", align_bytes=64)
-        nc.sync.dma_start(scale_table[0:32, :].bitcast(I32), x_scales.rearrange("o i c -> (o i) c").bitcast(I32))
-        nc.gpsimd.memset(scale_table[32:64, :].bitcast(I32), 0)
-        nc.vector.memset(scale_table[64:P, :].bitcast(I32), 0)
+        scale_table = keep.tile([P, T], U8, name="scale_table", tag="scales_then_given", align_bytes=64)
+        nc.sync.dma_start(scale_table[0:QUADRANT, :].bitcast(I32), x_scales.rearrange("o i c -> (o i) c").bitcast(I32))
+        nc.gpsimd.memset(scale_table[QUADRANT : 2 * QUADRANT, :].bitcast(I32), 0)
+        nc.vector.memset(scale_table[2 * QUADRANT : P, :].bitcast(I32), 0)
 
-        rows = []
-        for name, source in (("prior", prior), ("wgt", wgt)):
-            row = keep.tile([P, 2, 4], F32, name=name + "_row")
-            nc.scalar.dma_start(row[:], source[0].rearrange("(h n m) -> n h m", h=2, m=4))
-            rows.append(row)
-
-        w_raw = keep.tile([P, PASSES, 4, N], F32, name="w_raw")
-        nc.sync.dma_start(w_raw[:], w1.rearrange("(o p j) n -> p o j n", o=PASSES, j=4))
+        w_raw = keep.tile([P, PASSES, PACK, N], F32, name="w_raw")
+        nc.sync.dma_start(w_raw[:], w1.rearrange("(o p j) n -> p o j n", o=PASSES, j=PACK))
 
         word_table = []
         for o in range(PASSES):
@@ -56,107 +61,114 @@ def tile_picked_yprot_nlog_p_kernel(tc, x_words, x_scales, w1, prior, wgt, offs,
             nc.sync.dma_start(table[:], x_words[o].rearrange("p c r -> p (c r)").bitcast(I32))
             word_table.append(table)
 
-        identity = keep.tile([P, P], F32, name="identity")
-        make_identity(nc, identity[:])
-        spread = []
-        for index, row in enumerate(rows):
-            banks = []
-            for h in range(2):
-                bank = psum.tile([P, 4, P], F32, name="spread%d_%d" % (index, h))
-                for m in range(4):
-                    nc.tensor.transpose(bank[:, m, :], row[:, h, m : m + 1].to_broadcast([P, P]), identity[:])
-                banks.append(bank)
-            spread.append(banks)
+        planes = [keep.tile([P, S], U8, name="plane%d" % o, align_bytes=64) for o in range(PASSES)]
+        for plane in planes:
+            nc.gpsimd.memset(plane[:].bitcast(I32), 0)
 
-        def spread_block(index, b):
-            n0 = (b % 2) * (BLOCK // 4)
-            return spread[index][b // 2][:].rearrange("p m n -> p n m")[:, n0 : n0 + BLOCK // 4, :]
-
-        def by_four(ap):
-            return ap.rearrange("p (n m) -> p n m", m=4)
-
-        w_bf = keep.tile([P, PASSES * N * 4], BF16, name="w_bf", align_bytes=64)
+        w_bf = keep.tile([P, PASSES * N * PACK], BF16, name="w_bf", align_bytes=64)
         nc.scalar.activation(
-            w_bf[:].rearrange("p (o n j) -> p o n j", o=PASSES, j=4),
+            w_bf[:].rearrange("p (o n j) -> p o n j", o=PASSES, j=PACK),
             w_raw[:].rearrange("p o j n -> p o n j"),
             ACT.Copy,
         )
 
         picked_bytes = keep.tile([P, S], U8, name="picked_bytes", align_bytes=64)
         nc.vector.tensor_copy(picked_bytes[:], scale_table[:].indirect(offsets[:]))
-        planes = keep.tile([P, S], U8, name="planes", align_bytes=64)
-        nc.vector.tensor_copy(planes[:].bitcast(I32), picked_bytes[:].bitcast(I32))
         for o in range(PASSES):
-            for q in range(4):
-                source, target = 16 * o + 4 * q, 32 * q + 4 * o
+            for q in range(P // QUADRANT):
+                source, target = ROWS * (P // QUADRANT * o + q), QUADRANT * q
                 if source != target:
-                    nc.scalar.dma_start(
-                        planes[target : target + 4, :].bitcast(I32), picked_bytes[source : source + 4, :].bitcast(I32)
+                    nc.sync.dma_start(
+                        planes[o][target : target + ROWS, :].bitcast(I32),
+                        picked_bytes[source : source + ROWS, :].bitcast(I32),
                     )
+        nc.vector.tensor_copy(planes[0][0:QUADRANT, :].bitcast(I32), picked_bytes[0:QUADRANT, :].bitcast(I32))
+
+        given = keep.tile([P, 2 * S], F32, name="given", tag="scales_then_given", align_bytes=64)
+        prior_sb, wgt_sb = given[:, :S], given[:, S:]
+        for g in range(S // GATHER):
+            nc.sync.dma_start(prior_sb[:, g * GATHER : (g + 1) * GATHER], prior[:, g * GATHER : (g + 1) * GATHER])
+        nc.sync.dma_start(wgt_sb, wgt)
 
         w_codes = keep.tile([P, PASSES * N], U32, name="w_codes", align_bytes=64)
         w_scales = keep.tile([P, PASSES * N], U8, name="w_scales", align_bytes=64)
         nc.vector.quantize_mx(w_codes[:].bitcast(FP8X4), w_scales[:], w_bf[:])
 
-        y = [psum.tile([P, BLOCK], F32, name="y%d" % b) for b in range(BLOCKS)]
+        picked_words = {}
         for o in range(PASSES):
             for g in range(S // GATHER):
-                picked = keep.tile([P, GATHER], U32, name="picked%d_%d" % (o, g), align_bytes=64)
-                nc.vector.tensor_copy(
-                    picked[:],
-                    word_table[o][:].bitcast(U32).indirect(offsets[:, g * GATHER // 16 : (g + 1) * GATHER // 16]),
-                )
-                for i in range(GATHER // BLOCK):
-                    b = g * (GATHER // BLOCK) + i
-                    nc.tensor.matmul_mx(
-                        y[b][:],
-                        lhsT=w_codes[:, o * N : (o + 1) * N].bitcast(FP8X4),
-                        lhsT_scale=w_scales[:, o * N : (o + 1) * N],
-                        rhs=picked[:, i * BLOCK : (i + 1) * BLOCK].bitcast(FP8X4),
-                        rhs_scale=planes[4 * o : P, b * BLOCK : (b + 1) * BLOCK],
-                        start=(o == 0),
-                        stop=(o == PASSES - 1),
-                    )
+                picked_words[o, g] = keep.tile([P, GATHER], U32, name="picked_words%d_%d" % (o, g), align_bytes=64)
+                entries = offsets[:, g * GATHER // STRIPE : (g + 1) * GATHER // STRIPE]
+                nc.vector.tensor_copy(picked_words[o, g][:], word_table[o][:].bitcast(U32).indirect(entries))
 
-        def cols(b):
-            return slice(b * BLOCK, (b + 1) * BLOCK)
+        y = [psum.tile([P, BLOCK], F32, name="y%d" % b) for b in range(BLOCKS)]
 
-        def fresh(name, b, width=BLOCK):
-            return keep.tile([P, width], F32, name="%s%d" % (name, b))
+        def product(o, b):
+            g, i = divmod(b, PER_GATHER)
+            nc.tensor.matmul_mx(
+                y[b][:],
+                lhsT=w_codes[:, o * N : (o + 1) * N].bitcast(FP8X4),
+                lhsT_scale=w_scales[:, o * N : (o + 1) * N],
+                rhs=picked_words[o, g][:, cols(i)].bitcast(FP8X4),
+                rhs_scale=planes[o][:, cols(b)],
+                start=(o == 0),
+                stop=(o == PASSES - 1),
+            )
+
+        for b in range(BLOCKS - 1):
+            product(0, b)
+        for b in range(PER_GATHER):
+            product(1, b)
+        product(0, BLOCKS - 1)
+        for b in range(PER_GATHER, BLOCKS):
+            product(1, b)
 
         root = math.sqrt(0.7)
-        square, expo, part, logit, th = {}, {}, {}, {}, {}
-        for b in range(BLOCKS):
-            square[b] = fresh("square", b)
-            nc.scalar.activation(square[b][:], y[b][:], ACT.Square, bias=-root * CENTRE, scale=root)
-            expo[b] = fresh("expo", b)
-            nc.scalar.activation(expo[b][:], y[b][:], ACT.Exp, bias=-1.2 * 0.3, scale=-1.2)
-        for pair in range(BLOCKS // 2):
-            for b in (2 * pair, 2 * pair + 1):
+        square, expo, part, logit, tanh_half = {}, {}, {}, {}, {}
+        twos = [range(g * PER_GATHER, (g + 1) * PER_GATHER) for g in range(S // GATHER)]
+        for two in twos:
+            for b in two:
+                square[b] = fresh("square", b)
+                nc.scalar.activation(square[b][:], y[b][:], ACT.Square, bias=-root * CENTRE, scale=root)
+            for b in two:
+                expo[b] = fresh("expo", b)
+                nc.scalar.activation(expo[b][:], y[b][:], ACT.Exp, bias=-1.2 * 0.3, scale=-1.2)
+        for two in twos:
+            for b in two:
                 part[b] = fresh("part", b)
-                nc.vector.tensor_tensor(by_four(part[b][:]), spread_block(0, b), by_four(square[b][:]), ALU.subtract)
-            for b in (2 * pair, 2 * pair + 1):
+                nc.vector.tensor_tensor(part[b][:], prior_sb[:, cols(b)], square[b][:], ALU.subtract)
+            for b in two:
                 logit[b] = fresh("logit", b)
                 nc.vector.tensor_tensor(logit[b][:], part[b][:], expo[b][:], ALU.add)
         for b in range(BLOCKS):
-            th[b] = fresh("th", b)
-            nc.scalar.activation(th[b][:], logit[b][:], ACT.Tanh, bias=0.5 * OFFSET, scale=0.5)
+            tanh_half[b] = fresh("tanh_half", b)
+            nc.scalar.activation(tanh_half[b][:], logit[b][:], ACT.Tanh, bias=0.5 * OFFSET, scale=0.5)
 
-        HALF = 2 * BLOCK
-        for h in range(S // HALF):
-            twice_p = fresh("twice_p", h, HALF)
-            for i in range(2):
-                b = 2 * h + i
-                nc.vector.scalar_tensor_tensor(
-                    by_four(twice_p[:, cols(i)]), by_four(th[b][:]), 1.0, spread_block(1, b), ALU.add, ALU.mult
-                )
-            pairs = twice_p[:].rearrange("p (v d) -> p v d", d=2)
-            cross = fresh("cross", h)
-            nc.vector.scalar_tensor_tensor(cross[:], pairs[:, :, 0], -2.0, pairs[:, :, 1], ALU.add, ALU.mult)
-            excess = fresh("excess", h)
-            nc.vector.scalar_tensor_tensor(excess[:], pairs[:, :, 0], -2.0, cross[:], ALU.mult, ALU.add)
-            log_q = keep.tile([P, BLOCK], F32, name="logit%d" % (BLOCKS - 1 - h))
-            nc.scalar.activation(log_q[:], excess[:], ACT.Ln, bias=1.0, scale=0.25)
-            result = fresh("result", h)
-            nc.vector.tensor_scalar(result[:], log_q[:], -1.0, None, ALU.mult)
-            nc.sync.dma_start(out[:, cols(h)], result[:])
+        twice_p = keep.tile([P, S], F32, name="twice_p")
+        for b in range(BLOCKS):
+            nc.vector.scalar_tensor_tensor(
+                twice_p[:, cols(b)], tanh_half[b][:], 1.0, wgt_sb[:, cols(b)], ALU.add, ALU.mult
+            )
+
+        pairs = twice_p[:].rearrange("p (v d) -> p v d", d=2)
+        rest = slice(PROTEINS, S // 2)
+        cross = keep.tile([P, S // 2], F32, name="cross")
+        nc.vector.scalar_tensor_tensor(cross[:, rest], pairs[:, rest, 0], -2.0, pairs[:, rest, 1], ALU.add, ALU.mult)
+        parts = [slice(PROTEINS, (BLOCKS - 1) * PROTEINS), slice((BLOCKS - 1) * PROTEINS, S // 2)]
+        excess = [fresh("excess", h, v.stop - v.start) for h, v in enumerate(parts)]
+        for h, v in enumerate(parts):
+            nc.vector.scalar_tensor_tensor(excess[h][:], pairs[:, v, 0], -2.0, cross[:, v], ALU.mult, ALU.add)
+
+        log_factor = fresh("logit", BLOCKS - 1)
+        nc.scalar.activation(log_factor[:], twice_p[:, cols(0)], ACT.Ln, bias=1.0, scale=-0.5)
+        log_pairs = log_factor[:].rearrange("p (v d) -> p v d", d=2)
+        first = keep.tile([P, PROTEINS], F32, name="first")
+        nc.vector.scalar_tensor_tensor(first[:], log_pairs[:, :, 0], -1.0, log_pairs[:, :, 1], ALU.mult, ALU.subtract)
+        nc.sync.dma_start(out[:, :PROTEINS], first[:])
+
+        for h, v in enumerate(parts):
+            log_product = fresh("log_product", h, v.stop - v.start)
+            nc.scalar.activation(log_product[:], excess[h][:], ACT.Ln, bias=1.0, scale=0.25)
+            result = fresh("result", h, v.stop - v.start)
+            nc.vector.tensor_scalar(result[:], log_product[:], -1.0, None, ALU.mult)
+            nc.sync.dma_start(out[:, v], result[:])

import math
from contextlib import ExitStack

import concourse.mybir as mybir

K, T, S, N = 1024, 4096, 1024, 128
P = 128
PACK = 4
PASSES = K // (P * PACK)
FLOPS = 2 * K * S * N

F32 = mybir.dt.float32
BF16 = mybir.dt.bfloat16
I32 = mybir.dt.int32
U32 = mybir.dt.uint32
U16 = mybir.dt.uint16
U8 = mybir.dt.uint8
FP8X4 = mybir.dt.float8_e4m3fn_x4
ACT = mybir.ActivationFunctionType
ALU = mybir.AluOpType

STRIPE = 16
QUADRANT = 32
ROWS = 4
GATHER = 512
BLOCK = 256
BLOCKS = S // BLOCK
PER_GATHER = GATHER // BLOCK
PROTEINS = BLOCK // 2

CENTRE = (2 * 0.7 * 0.8 + 1.2) / (2 * 0.7)
OFFSET = 0.7 * CENTRE * CENTRE - 0.7 * 0.8 * 0.8 + 1.2 * 0.3


def tile_picked_yprot_nlog_p_kernel(tc, x_words, x_scales, w1, prior, wgt, offs, out):
    nc = tc.nc
    with ExitStack() as ctx:
        keep = ctx.enter_context(tc.tile_pool(name="keep", bufs=1))
        psum = ctx.enter_context(tc.psum_pool(name="psum", bufs=1))

        def cols(b):
            return slice(b * BLOCK, (b + 1) * BLOCK)

        def fresh(name, index, width=BLOCK):
            return keep.tile([P, width], F32, name="%s%d" % (name, index))

        offsets = keep.tile([P, S // STRIPE], U16, name="offsets")
        nc.sync.dma_start(offsets[:], offs)

        scale_table = keep.tile([P, T], U8, name="scale_table", tag="scales_then_given", align_bytes=64)
        nc.sync.dma_start(scale_table[0:QUADRANT, :].bitcast(I32), x_scales.rearrange("o i c -> (o i) c").bitcast(I32))
        nc.gpsimd.memset(scale_table[QUADRANT : 2 * QUADRANT, :].bitcast(I32), 0)
        nc.vector.memset(scale_table[2 * QUADRANT : P, :].bitcast(I32), 0)

        w_raw = keep.tile([P, PASSES, PACK, N], F32, name="w_raw")
        nc.sync.dma_start(w_raw[:], w1.rearrange("(o p j) n -> p o j n", o=PASSES, j=PACK))

        word_table = []
        for o in range(PASSES):
            table = keep.tile([P, T], I32, name="word_table%d" % o, align_bytes=64)
            nc.sync.dma_start(table[:], x_words[o].rearrange("p c r -> p (c r)").bitcast(I32))
            word_table.append(table)

        planes = [keep.tile([P, S], U8, name="plane%d" % o, align_bytes=64) for o in range(PASSES)]
        for plane in planes:
            nc.gpsimd.memset(plane[:].bitcast(I32), 0)

        w_bf = keep.tile([P, PASSES * N * PACK], BF16, name="w_bf", align_bytes=64)
        nc.scalar.activation(
            w_bf[:].rearrange("p (o n j) -> p o n j", o=PASSES, j=PACK),
            w_raw[:].rearrange("p o j n -> p o n j"),
            ACT.Copy,
        )

        picked_bytes = keep.tile([P, S], U8, name="picked_bytes", align_bytes=64)
        nc.vector.tensor_copy(picked_bytes[:], scale_table[:].indirect(offsets[:]))
        for o in range(PASSES):
            for q in range(P // QUADRANT):
                source, target = ROWS * (P // QUADRANT * o + q), QUADRANT * q
                if source != target:
                    nc.sync.dma_start(
                        planes[o][target : target + ROWS, :].bitcast(I32),
                        picked_bytes[source : source + ROWS, :].bitcast(I32),
                    )
        nc.vector.tensor_copy(planes[0][0:QUADRANT, :].bitcast(I32), picked_bytes[0:QUADRANT, :].bitcast(I32))

        given = keep.tile([P, 2 * S], F32, name="given", tag="scales_then_given", align_bytes=64)
        prior_sb, wgt_sb = given[:, :S], given[:, S:]
        for g in range(S // GATHER):
            nc.sync.dma_start(prior_sb[:, g * GATHER : (g + 1) * GATHER], prior[:, g * GATHER : (g + 1) * GATHER])
        nc.sync.dma_start(wgt_sb, wgt)

        w_codes = keep.tile([P, PASSES * N], U32, name="w_codes", align_bytes=64)
        w_scales = keep.tile([P, PASSES * N], U8, name="w_scales", align_bytes=64)
        nc.vector.quantize_mx(w_codes[:].bitcast(FP8X4), w_scales[:], w_bf[:])

        picked_words = {}
        for o in range(PASSES):
            for g in range(S // GATHER):
                picked_words[o, g] = keep.tile([P, GATHER], U32, name="picked_words%d_%d" % (o, g), align_bytes=64)
                entries = offsets[:, g * GATHER // STRIPE : (g + 1) * GATHER // STRIPE]
                nc.vector.tensor_copy(picked_words[o, g][:], word_table[o][:].bitcast(U32).indirect(entries))

        y = [psum.tile([P, BLOCK], F32, name="y%d" % b) for b in range(BLOCKS)]

        def product(o, b):
            g, i = divmod(b, PER_GATHER)
            nc.tensor.matmul_mx(
                y[b][:],
                lhsT=w_codes[:, o * N : (o + 1) * N].bitcast(FP8X4),
                lhsT_scale=w_scales[:, o * N : (o + 1) * N],
                rhs=picked_words[o, g][:, cols(i)].bitcast(FP8X4),
                rhs_scale=planes[o][:, cols(b)],
                start=(o == 0),
                stop=(o == PASSES - 1),
            )

        for b in range(BLOCKS - 1):
            product(0, b)
        for b in range(PER_GATHER):
            product(1, b)
        product(0, BLOCKS - 1)
        for b in range(PER_GATHER, BLOCKS):
            product(1, b)

        root = math.sqrt(0.7)
        square, expo, part, logit, tanh_half = {}, {}, {}, {}, {}
        twos = [range(g * PER_GATHER, (g + 1) * PER_GATHER) for g in range(S // GATHER)]
        for two in twos:
            for b in two:
                square[b] = fresh("square", b)
                nc.scalar.activation(square[b][:], y[b][:], ACT.Square, bias=-root * CENTRE, scale=root)
            for b in two:
                expo[b] = fresh("expo", b)
                nc.scalar.activation(expo[b][:], y[b][:], ACT.Exp, bias=-1.2 * 0.3, scale=-1.2)
        for two in twos:
            for b in two:
                part[b] = fresh("part", b)
                nc.vector.tensor_tensor(part[b][:], prior_sb[:, cols(b)], square[b][:], ALU.subtract)
            for b in two:
                logit[b] = fresh("logit", b)
                nc.vector.tensor_tensor(logit[b][:], part[b][:], expo[b][:], ALU.add)
        for b in range(BLOCKS):
            tanh_half[b] = fresh("tanh_half", b)
            nc.scalar.activation(tanh_half[b][:], logit[b][:], ACT.Tanh, bias=0.5 * OFFSET, scale=0.5)

        twice_p = keep.tile([P, S], F32, name="twice_p")
        for b in range(BLOCKS):
            nc.vector.scalar_tensor_tensor(
                twice_p[:, cols(b)], tanh_half[b][:], 1.0, wgt_sb[:, cols(b)], ALU.add, ALU.mult
            )

        pairs = twice_p[:].rearrange("p (v d) -> p v d", d=2)
        rest = slice(PROTEINS, S // 2)
        cross = keep.tile([P, S // 2], F32, name="cross")
        nc.vector.scalar_tensor_tensor(cross[:, rest], pairs[:, rest, 0], -2.0, pairs[:, rest, 1], ALU.add, ALU.mult)
        parts = [slice(PROTEINS, (BLOCKS - 1) * PROTEINS), slice((BLOCKS - 1) * PROTEINS, S // 2)]
        excess = [fresh("excess", h, v.stop - v.start) for h, v in enumerate(parts)]
        for h, v in enumerate(parts):
            nc.vector.scalar_tensor_tensor(excess[h][:], pairs[:, v, 0], -2.0, cross[:, v], ALU.mult, ALU.add)

        log_factor = fresh("logit", BLOCKS - 1)
        nc.scalar.activation(log_factor[:], twice_p[:, cols(0)], ACT.Ln, bias=1.0, scale=-0.5)
        log_pairs = log_factor[:].rearrange("p (v d) -> p v d", d=2)
        first = keep.tile([P, PROTEINS], F32, name="first")
        nc.vector.scalar_tensor_tensor(first[:], log_pairs[:, :, 0], -1.0, log_pairs[:, :, 1], ALU.mult, ALU.subtract)
        nc.sync.dma_start(out[:, :PROTEINS], first[:])

        for h, v in enumerate(parts):
            log_product = fresh("log_product", h, v.stop - v.start)
            nc.scalar.activation(log_product[:], excess[h][:], ACT.Ln, bias=1.0, scale=0.25)
            result = fresh("result", h, v.stop - v.start)
            nc.vector.tensor_scalar(result[:], log_product[:], -1.0, None, ALU.mult)
            nc.sync.dma_start(out[:, v], result[:])
